import numpy as np
import ml_dtypes


def mxq(x, axis, fmt="e4m3"):
    dtype, down = {"e4m3": (ml_dtypes.float8_e4m3fn, 7), "e5m2": (ml_dtypes.float8_e5m2, 14)}[fmt]
    v = np.moveaxis(np.asarray(x, np.float32).astype(ml_dtypes.bfloat16).astype(np.float64), axis, -1)
    blocks = v.reshape(v.shape[:-1] + (-1, 32))
    amax = np.abs(blocks).max(-1, keepdims=True)
    byte = np.maximum(np.where(amax > 0, np.frexp(amax)[1] - 1 + 127, 0) - down, 1)
    scale = np.exp2(byte - 127.0)
    codes = (blocks / scale).astype(np.float32).astype(dtype).astype(np.float64)
    return np.moveaxis((codes * scale).reshape(v.shape), -1, axis)


WIDE = False


def mx_kscale(k):
    if not WIDE:
        return np.ones(k)
    levels = np.array([10, -10, 5, -5, 0])
    if k % 512:
        return np.exp2(np.random.permutation(np.resize(levels, k // 32))).repeat(32)
    a = np.empty((k // 512, 16))
    for p in range(k // 512):
        a[p, :8] = np.random.permutation(np.resize(levels, 8))
        for g in range(8):
            far = levels[np.abs(levels - a[p, g]) >= 10]
            a[p, g + 8] = far[np.random.randint(len(far))]
    return np.exp2(a.ravel()).repeat(32)


def f64(x):
    return np.asarray(x).astype(np.float64)


def striped(idx):
    return np.tile(np.asarray(idx).reshape(-1, 16).T, (8, 1)).astype(np.uint16)


def unstriped(offs):
    return offs[:16].T.reshape(-1).astype(np.int64)


def striped8(idx):
    return np.asarray(idx).reshape(8, -1, 16).transpose(0, 2, 1).reshape(128, -1).astype(np.uint16)


def unstriped8(offs):
    return offs.reshape(8, 16, -1).transpose(0, 2, 1).reshape(8, -1).astype(np.int64)


def pick8(x, idx, run):
    r = np.arange(len(x))
    return x[r[:, None], idx[r % (8 * run) // run]]


E2M1 = np.array([0.0, 0.5, 1.0, 1.5, 2.0, 3.0, 4.0, 6.0, -0.0, -0.5, -1.0, -1.5, -2.0, -3.0, -4.0, -6.0])


def pack_weight(w, fmt):
    k, n = w.shape
    w = f64(np.asarray(w, np.float32).astype(ml_dtypes.bfloat16)).reshape(k // 32, 32, n)
    amax = np.abs(w).max(1)
    if fmt == "e4m3":
        byte = np.frexp(amax)[1] - 1 + 127 - 7
    else:
        mant, ex = np.frexp(amax / 6.0)
        byte = np.where(mant > 0.5, ex, ex - 1) + 127
    byte = np.clip(np.where(amax > 0, byte, 1), 1, 254)
    scaled = (w * np.exp2(127.0 - byte)[:, None, :]).reshape(k, n).astype(np.float32)
    by_word = np.ascontiguousarray(scaled.reshape(k // 512, 128, 4, n).transpose(0, 1, 3, 2))
    if fmt == "e4m3":
        words = by_word.astype(ml_dtypes.float8_e4m3fn).view(np.uint8)
    else:
        c = by_word.astype(ml_dtypes.float4_e2m1fn).view(np.uint8) & 0xF
        words = (c[..., 0::2] | (c[..., 1::2] << 4)).reshape(k // 512, 128, 2 * n)
    return np.ascontiguousarray(words), np.ascontiguousarray(byte.astype(np.uint8).reshape(k // 512, 16, n))


def unpack_weight(words, scales, fmt):
    g, _, n = scales.shape
    words = np.ascontiguousarray(words).reshape(g, 128, n, -1)
    if fmt == "e4m3":
        vals = words.view(ml_dtypes.float8_e4m3fn).astype(np.float64)
    else:
        nib = np.empty((g, 128, n, 4), np.uint8)
        nib[..., 0::2] = words & 0xF
        nib[..., 1::2] = words >> 4
        vals = E2M1[nib]
    vals = vals * np.repeat(np.exp2(scales.astype(np.float64) - 127.0), 8, axis=1)[..., None]
    return vals.transpose(0, 1, 3, 2).reshape(g * 512, n)


K, J, R, T, F, O, C, N = 512, 512, 512, 1024, 1024, 192, 256, 256


def setup_inputs():
    n = np.random.standard_normal
    idx = np.random.permutation(T)[:J]
    idx2 = np.random.permutation(F)[:R]
    idx3 = np.stack([np.random.permutation(J)[:O] for _ in range(8)])
    idx4 = np.stack([np.random.permutation(C)[:O] for _ in range(8)])
    idx5 = np.stack([np.random.permutation(J)[:C] for _ in range(8)])
    idx6 = np.random.permutation(T)[:C]
    fk = mx_kscale(K)
    fr = mx_kscale(R)
    tr = np.ones(F)
    tr[idx2] = fr
    xtp = pack_weight(n((K, T)) * fk[:, None], "e2m1")
    wtp = pack_weight(n((K, F)) * 1 / np.sqrt(K) / fk[:, None] * tr, "e2m1")
    wbp = pack_weight(n((R, N)) * 1 / np.sqrt(R) / fr[:, None], "e4m3")
    wsp = pack_weight(n((K, N)) * 1 / np.sqrt(K) / fk[:, None], "e4m3")
    return {
        "xt_words": xtp[0],
        "xt_scales": xtp[1],
        "wt_words": wtp[0],
        "wt_scales": wtp[1],
        "sa": (np.random.uniform(0.5, 1.6, (R, 1))).astype(np.float32),
        "sb": (np.random.uniform(0.5, 1.6, (R, 1))).astype(np.float32),
        "wb_words": wbp[0],
        "wb_scales": wbp[1],
        "ws_words": wsp[0],
        "ws_scales": wsp[1],
        "offs": striped(idx),
        "offs2": striped(idx2),
        "offs3": striped8(idx3),
        "offs4": striped8(idx4),
        "offs5": striped8(idx5),
        "offs6": striped(idx6),
    }


def reference(xt_words, xt_scales, wt_words, wt_scales, sa, sb, wb_words, wb_scales, ws_words, ws_scales, offs, offs2, offs3, offs4, offs5, offs6):
    idx = unstriped(offs)
    idx2 = unstriped(offs2)
    idx3 = unstriped8(offs3)
    idx4 = unstriped8(offs4)
    idx5 = unstriped8(offs5)
    idx6 = unstriped(offs6)
    xtu = unpack_weight(xt_words, xt_scales, "e2m1")
    wtu = unpack_weight(wt_words, wt_scales, "e2m1")
    wbu = unpack_weight(wb_words, wb_scales, "e4m3")
    wsu = unpack_weight(ws_words, ws_scales, "e4m3")
    wtidx2g = wtu[:, idx2]
    xtidxg = xtu[:, idx]
    a = wtidx2g.T @ xtidxg
    h1 = pick8(a, idx3, 64) * f64(sa)
    pw = np.zeros((R, C))
    pw[np.arange(R)[:, None], idx4[np.arange(R) % 512 // 64]] = h1
    hid = np.abs(pw - pick8(a, idx5, 64) * f64(sb))
    hidq = mxq(hid, 0, "e4m3")
    xtidx6g = xtu[:, idx6]
    y = wbu.T @ hidq + wsu.T @ xtidx6g
    return y

@@ -1,0 +1,179 @@
+from contextlib import ExitStack
+
+import concourse.mybir as mybir
+
+K, J, R, T, F, O, C, N = 512, 512, 512, 1024, 1024, 192, 256, 256
+FLOPS = 2 * K * R * J + 2 * R * N * C + 2 * K * N * C
+
+F32 = mybir.dt.float32
+BF16 = mybir.dt.bfloat16
+I32 = mybir.dt.int32
+U32 = mybir.dt.uint32
+U16 = mybir.dt.uint16
+U8 = mybir.dt.uint8
+FP8X4 = mybir.dt.float8_e4m3fn_x4
+FP4X4 = mybir.dt.float4_e2m1fn_x4
+ALU = mybir.AluOpType
+COPY = mybir.ActivationFunctionType.Copy
+
+P = 128
+PACK = 4
+GROUP = 16
+HALF = C // 2
+
+
+def tile_picked_tokens_store_one_wholepage_further_plain_kernel(
+    tc, xt_words, xt_scales, wt_words, wt_scales, sa, sb, wb_words, wb_scales, ws_words, ws_scales,
+    offs, offs2, offs3, offs4, offs5, offs6, out,
+):
+    nc = tc.nc
+    with ExitStack() as ctx:
+        keep = ctx.enter_context(tc.tile_pool(name="keep", bufs=1))
+        psum = ctx.enter_context(tc.psum_pool(name="psum", bufs=1))
+
+        def sbuf(name, shape, dtype, tag=None):
+            return keep.tile(shape, dtype, name=name, tag=tag or name, align_bytes=64)
+
+        def load_list(name, src):
+            tile = sbuf(name, list(src.shape), U16)
+            nc.sync.dma_start(tile[:], src)
+            return tile
+
+        def load_words(name, src, shape, dtype):
+            tile = sbuf(name, shape, dtype)
+            nc.sync.dma_start(tile[:].bitcast(I32), src.bitcast(I32))
+            return tile
+
+        def cleared_plane(name, width, engine):
+            plane = sbuf(name, [P, width], U8)
+            engine.memset(plane[:].bitcast(I32), 0)
+            return plane
+
+        def load_plane(plane, src):
+            for q in range(4):
+                nc.sync.dma_start(plane[32 * q:32 * q + 4, :].bitcast(I32), src[0, 4 * q:4 * q + 4, :].bitcast(I32))
+
+        wt_plane = cleared_plane("wt_plane", F, nc.gpsimd)
+        xt_plane = cleared_plane("xt_plane", T, nc.gpsimd)
+        pw = [sbuf("pw%d" % t, [P, C], F32) for t in range(PACK)]
+        for t in range(PACK):
+            nc.gpsimd.memset(pw[t][:], 0.0)
+        ws_plane = cleared_plane("ws_plane", N, nc.gpsimd)
+        wb_plane = cleared_plane("wb_plane", N, nc.gpsimd)
+
+        wt_win = load_words("wt_win", wt_words[0], [P, F], U16)
+        list2 = load_list("list2", offs2)
+        list1 = load_list("list1", offs)
+        xt_win = load_words("xt_win", xt_words[0], [P, T], U16)
+        load_plane(wt_plane, wt_scales)
+        load_plane(xt_plane, xt_scales)
+        list3 = load_list("list3", offs3)
+        sa_t = sbuf("sa_t", [P, PACK], F32)
+        nc.sync.dma_start(sa_t[:], sa.rearrange("(p t) o -> p (t o)", t=PACK))
+        list5 = load_list("list5", offs5)
+        sb_t = sbuf("sb_t", [P, PACK], F32)
+        nc.sync.dma_start(sb_t[:], sb.rearrange("(p t) o -> p (t o)", t=PACK))
+        list4 = load_list("list4", offs4)
+        list6 = load_list("list6", offs6)
+        ws_codes = load_words("ws_codes", ws_words[0].rearrange("p n t -> p (n t)"), [P, N], U32)
+        load_plane(ws_plane, ws_scales)
+        wb_codes = load_words("wb_codes", wb_words[0].rearrange("p n t -> p (n t)"), [P, N], U32)
+        load_plane(wb_plane, wb_scales)
+
+        wt_got = sbuf("wt_got", [P, R], U16)
+        nc.vector.tensor_copy(wt_got[:], wt_win[:].indirect(list2[:]))
+        wt_dealt = {}
+        wt_bytes = wt_got[:].bitcast(U8).rearrange("p (m t b) -> p m t b", t=PACK, b=2)
+
+        def deal(t0, t1):
+            tile = sbuf("wt_dealt%d" % t0, [P, t1 - t0, 2 * P], U8, tag="wt_dealt")
+            nc.vector.tensor_copy(
+                tile[:].rearrange("p t (m b) -> p t m b", b=2), wt_bytes[:, :, t0:t1, :].rearrange("p m t b -> p t m b"))
+            for t in range(t0, t1):
+                wt_dealt[t] = tile[:, t - t0, :]
+
+        wt_sc = sbuf("wt_sc", [P, PACK, P], U8)
+        x_codes = sbuf("x_codes", [P, J], U16)
+        x_sc = sbuf("x_sc", [P, J], U8)
+        a = [sbuf("a%d" % t, [P, J], F32) for t in range(PACK)]
+
+        def first_product(t, cols, tag):
+            bank = psum.tile([P, cols.stop - cols.start], F32, name="acc_" + tag, tag=tag)
+            nc.tensor.matmul_mx(
+                bank[:], lhsT=wt_dealt[t].bitcast(FP4X4), lhsT_scale=wt_sc[:, t, :],
+                rhs=x_codes[:, cols].bitcast(U8).bitcast(FP4X4), rhs_scale=x_sc[:, cols], start=True, stop=True)
+            return bank
+
+        deal(0, 1)
+        nc.vector.tensor_copy(x_codes[:], xt_win[:].indirect(list1[:]))
+        nc.vector.tensor_copy(wt_sc[:].rearrange("p t m -> p m t"), wt_plane[:].indirect(list2[:]))
+        for i, cols in enumerate((slice(0, J // 2), slice(J // 2, J))):
+            entries = list1[:, cols.start // GROUP:cols.stop // GROUP]
+            nc.vector.tensor_copy(x_sc[:, cols], xt_plane[:].indirect(entries))
+            bank = first_product(0, cols, "a_part%d" % i)
+            nc.scalar.copy(a[0][:, cols], bank[:])
+        for t in range(1, PACK):
+            if t < 3:
+                deal(t, 2 * t)
+            bank = first_product(t, slice(0, J), ("a_tile1", "a_tile2", "a_part0")[t - 1])
+            nc.vector.tensor_copy(a[t][:], bank[:])
+
+        x6_codes = sbuf("x6_codes", [P, C], U16, tag="wt_got")
+        x6_sc = sbuf("x6_sc", [P, C], U8, tag="wt_dealt")
+        nc.vector.tensor_copy(x6_codes[:], xt_win[:].indirect(list6[:]))
+        nc.vector.tensor_copy(x6_sc[:], xt_plane[:].indirect(list6[:]))
+        y = [[psum.tile([P, HALF], F32, name="y%d%d" % (h, b)) for b in range(2)] for h in range(2)]
+        for h in range(2):
+            cols = slice(h * HALF, (h + 1) * HALF)
+            for b in range(2):
+                rows = slice(b * P, (b + 1) * P)
+                nc.tensor.matmul_mx(
+                    y[h][b][:], lhsT=ws_codes[:, rows].bitcast(FP8X4), lhsT_scale=ws_plane[:, rows],
+                    rhs=x6_codes[:, cols].bitcast(U8).bitcast(FP4X4), rhs_scale=x6_sc[:, cols], start=True, stop=False)
+
+        h1 = [sbuf("h1_%d" % t, [P, O], F32) for t in range(PACK)]
+        held = {(0, 0): "wt_sc", (0, 1): "x_codes"}
+        diff = [[sbuf("diff%d%d" % (u, h), [P, 2, HALF], F32, tag=held.get((u, h))) for h in range(2)] for u in range(2)]
+        hid = [sbuf("hid%d" % h, [P, HALF, PACK], BF16) for h in range(2)]
+
+        def fetch5(t, cols, tag):
+            tile = sbuf("g5_%d_%d" % (t, cols.start), [P, cols.stop - cols.start], F32, tag=tag)
+            entries = list5[:, cols.start // GROUP:cols.stop // GROUP]
+            nc.scalar.activation(tile[:], a[t][:].indirect(entries), COPY, scale=sb_t[:, t:t + 1])
+            return tile
+
+        halves = (slice(0, HALF), slice(HALF, C))
+        for t in range(PACK):
+            last = t == PACK - 1
+            nc.scalar.activation(h1[t][:], a[t][:].indirect(list3[:]), COPY, scale=sa_t[:, t:t + 1])
+            first = fetch5(t, halves[0] if last else slice(0, C), "g5_%d" % t)
+            nc.scalar.activation(pw[t][:].indirect(list4[:]), h1[t][:], COPY)
+            for h in range(2):
+                if not last:
+                    g = first[:, halves[h]]
+                elif h == 0:
+                    g = first[:]
+                else:
+                    g = fetch5(t, halves[1], "g5_%d" % (t - 1))[:]
+                nc.vector.tensor_tensor(diff[t // 2][h][:, t % 2, :], pw[t][:, halves[h]], g, ALU.subtract)
+            if t % 2 == 1:
+                for h in range(2):
+                    pair = diff[t // 2][h][:].rearrange("p t c -> p c t")
+                    nc.vector.scalar_tensor_tensor(hid[h][:, :, t - 1:t + 1], pair, -1.0, pair, ALU.mult, ALU.max)
+
+        for h in range(2):
+            codes = sbuf("hid_codes%d" % h, [P, HALF], U32)
+            scales = sbuf("hid_sc%d" % h, [P, HALF], U8)
+            nc.vector.quantize_mx(codes[:].bitcast(FP8X4), scales[:], hid[h][:].rearrange("p c t -> p (c t)"))
+            for b in range(2):
+                rows = slice(b * P, (b + 1) * P)
+                nc.tensor.matmul_mx(
+                    y[h][b][:], lhsT=wb_codes[:, rows].bitcast(FP8X4), lhsT_scale=wb_plane[:, rows],
+                    rhs=codes[:].bitcast(FP8X4), rhs_scale=scales[:], start=False, stop=True)
+                res = sbuf("res%d%d" % (h, b), [P, HALF], F32)
+                if b == 0:
+                    nc.scalar.copy(res[:], y[h][b][:])
+                    nc.scalar.dma_start(out[rows, h * HALF:(h + 1) * HALF], res[:])
+                else:
+                    nc.vector.tensor_copy(res[:], y[h][b][:])
+                    nc.sync.dma_start(out[rows, h * HALF:(h + 1) * HALF], res[:])

@@ -15,6 +15,7 @@ FP8X4 = mybir.dt.float8_e4m3fn_x4
 FP4X4 = mybir.dt.float4_e2m1fn_x4
 ALU = mybir.AluOpType
 COPY = mybir.ActivationFunctionType.Copy
+ABS = mybir.ActivationFunctionType.Abs
 
 P = 128
 PACK = 4
@@ -53,13 +54,13 @@ def tile_picked_tokens_store_one_wholepage_further_plain_kernel(
             for q in range(4):
                 nc.sync.dma_start(plane[32 * q:32 * q + 4, :].bitcast(I32), src[0, 4 * q:4 * q + 4, :].bitcast(I32))
 
-        wt_plane = cleared_plane("wt_plane", F, nc.gpsimd)
+        wt_plane = cleared_plane("wt_plane", F, nc.vector)
         xt_plane = cleared_plane("xt_plane", T, nc.gpsimd)
         pw = [sbuf("pw%d" % t, [P, C], F32) for t in range(PACK)]
         for t in range(PACK):
-            nc.gpsimd.memset(pw[t][:], 0.0)
-        ws_plane = cleared_plane("ws_plane", N, nc.gpsimd)
-        wb_plane = cleared_plane("wb_plane", N, nc.gpsimd)
+            nc.vector.memset(pw[t][:], 0.0)
+        ws_plane = cleared_plane("ws_plane", N, nc.vector)
+        wb_plane = cleared_plane("wb_plane", N, nc.vector)
 
         wt_win = load_words("wt_win", wt_words[0], [P, F], U16)
         list2 = load_list("list2", offs2)
@@ -69,10 +70,10 @@ def tile_picked_tokens_store_one_wholepage_further_plain_kernel(
         load_plane(xt_plane, xt_scales)
         list3 = load_list("list3", offs3)
         sa_t = sbuf("sa_t", [P, PACK], F32)
-        nc.sync.dma_start(sa_t[:], sa.rearrange("(p t) o -> p (t o)", t=PACK))
+        nc.gpsimd.dma_start(sa_t[:], sa.rearrange("(p t) o -> p (t o)", t=PACK))
         list5 = load_list("list5", offs5)
         sb_t = sbuf("sb_t", [P, PACK], F32)
-        nc.sync.dma_start(sb_t[:], sb.rearrange("(p t) o -> p (t o)", t=PACK))
+        nc.gpsimd.dma_start(sb_t[:], sb.rearrange("(p t) o -> p (t o)", t=PACK))
         list4 = load_list("list4", offs4)
         list6 = load_list("list6", offs6)
         ws_codes = load_words("ws_codes", ws_words[0].rearrange("p n t -> p (n t)"), [P, N], U32)
@@ -86,9 +87,8 @@ def tile_picked_tokens_store_one_wholepage_further_plain_kernel(
         wt_bytes = wt_got[:].bitcast(U8).rearrange("p (m t b) -> p m t b", t=PACK, b=2)
 
         def deal(t0, t1):
-            tile = sbuf("wt_dealt%d" % t0, [P, t1 - t0, 2 * P], U8, tag="wt_dealt")
-            nc.vector.tensor_copy(
-                tile[:].rearrange("p t (m b) -> p t m b", b=2), wt_bytes[:, :, t0:t1, :].rearrange("p m t b -> p t m b"))
+            tile = sbuf("wt_dealt%d" % t0, [P, t1 - t0, P], U16, tag="wt_dealt")
+            nc.vector.tensor_copy(tile[:], wt_got[:].rearrange("p (m t) -> p t m", t=PACK)[:, t0:t1, :])
             for t in range(t0, t1):
                 wt_dealt[t] = tile[:, t - t0, :]
 
@@ -100,29 +100,31 @@ def tile_picked_tokens_store_one_wholepage_further_plain_kernel(
         def first_product(t, cols, tag):
             bank = psum.tile([P, cols.stop - cols.start], F32, name="acc_" + tag, tag=tag)
             nc.tensor.matmul_mx(
-                bank[:], lhsT=wt_dealt[t].bitcast(FP4X4), lhsT_scale=wt_sc[:, t, :],
+                bank[:], lhsT=wt_dealt[t].bitcast(U8).bitcast(FP4X4), lhsT_scale=wt_sc[:, t, :],
                 rhs=x_codes[:, cols].bitcast(U8).bitcast(FP4X4), rhs_scale=x_sc[:, cols], start=True, stop=True)
             return bank
 
-        deal(0, 1)
         nc.vector.tensor_copy(x_codes[:], xt_win[:].indirect(list1[:]))
+        deal(0, 1)
         nc.vector.tensor_copy(wt_sc[:].rearrange("p t m -> p m t"), wt_plane[:].indirect(list2[:]))
-        for i, cols in enumerate((slice(0, J // 2), slice(J // 2, J))):
+        for i, cols in enumerate((slice(0, 256), slice(256, 384), slice(384, J))):
             entries = list1[:, cols.start // GROUP:cols.stop // GROUP]
             nc.vector.tensor_copy(x_sc[:, cols], xt_plane[:].indirect(entries))
             bank = first_product(0, cols, "a_part%d" % i)
-            nc.scalar.copy(a[0][:, cols], bank[:])
+            if cols.stop < J:
+                nc.scalar.copy(a[0][:, cols], bank[:])
+            else:
+                nc.vector.tensor_copy(a[0][:, cols], bank[:])
+        deal(1, PACK)
         for t in range(1, PACK):
-            if t < 3:
-                deal(t, 2 * t)
-            bank = first_product(t, slice(0, J), ("a_tile1", "a_tile2", "a_part0")[t - 1])
+            bank = first_product(t, slice(0, J), "a_tile%d" % t)
             nc.vector.tensor_copy(a[t][:], bank[:])
 
         x6_codes = sbuf("x6_codes", [P, C], U16, tag="wt_got")
         x6_sc = sbuf("x6_sc", [P, C], U8, tag="wt_dealt")
         nc.vector.tensor_copy(x6_codes[:], xt_win[:].indirect(list6[:]))
         nc.vector.tensor_copy(x6_sc[:], xt_plane[:].indirect(list6[:]))
-        y = [[psum.tile([P, HALF], F32, name="y%d%d" % (h, b)) for b in range(2)] for h in range(2)]
+        y = [[psum.tile([P, HALF], F32, name="y%d%d" % (h, b), tag=("a_part%d" % b if h else "y%d" % b)) for b in range(2)] for h in range(2)]
         for h in range(2):
             cols = slice(h * HALF, (h + 1) * HALF)
             for b in range(2):
@@ -131,35 +133,42 @@ def tile_picked_tokens_store_one_wholepage_further_plain_kernel(
                     y[h][b][:], lhsT=ws_codes[:, rows].bitcast(FP8X4), lhsT_scale=ws_plane[:, rows],
                     rhs=x6_codes[:, cols].bitcast(U8).bitcast(FP4X4), rhs_scale=x6_sc[:, cols], start=True, stop=False)
 
-        h1 = [sbuf("h1_%d" % t, [P, O], F32) for t in range(PACK)]
         held = {(0, 0): "wt_sc", (0, 1): "x_codes"}
         diff = [[sbuf("diff%d%d" % (u, h), [P, 2, HALF], F32, tag=held.get((u, h))) for h in range(2)] for u in range(2)]
         hid = [sbuf("hid%d" % h, [P, HALF, PACK], BF16) for h in range(2)]
 
-        def fetch5(t, cols, tag):
-            tile = sbuf("g5_%d_%d" % (t, cols.start), [P, cols.stop - cols.start], F32, tag=tag)
+        def fetch5(t, cols, dst):
             entries = list5[:, cols.start // GROUP:cols.stop // GROUP]
-            nc.scalar.activation(tile[:], a[t][:].indirect(entries), COPY, scale=sb_t[:, t:t + 1])
-            return tile
+            nc.scalar.activation(dst, a[t][:].indirect(entries), COPY, scale=sb_t[:, t:t + 1])
 
         halves = (slice(0, HALF), slice(HALF, C))
         for t in range(PACK):
             last = t == PACK - 1
-            nc.scalar.activation(h1[t][:], a[t][:].indirect(list3[:]), COPY, scale=sa_t[:, t:t + 1])
-            first = fetch5(t, halves[0] if last else slice(0, C), "g5_%d" % t)
-            nc.scalar.activation(pw[t][:].indirect(list4[:]), h1[t][:], COPY)
+            if t == 0:
+                h1 = sbuf("h1_first", [P, O], F32, tag="fetched")[:]
+                g5 = sbuf("g5_first", [P, C], F32)[:]
+            else:
+                if t == 1:
+                    rest = sbuf("fetched_rest", [P, PACK - 1, O + C], F32, tag="fetched")
+                before = g5
+                h1, g5 = rest[:, t - 1, :O], rest[:, t - 1, O:]
+            nc.scalar.activation(h1, a[t][:].indirect(list3[:]), COPY, scale=sa_t[:, t:t + 1])
+            cols = halves[0] if last else slice(0, C)
+            fetch5(t, cols, g5[:, cols])
+            nc.scalar.activation(pw[t][:].indirect(list4[:]), h1, COPY)
             for h in range(2):
-                if not last:
-                    g = first[:, halves[h]]
-                elif h == 0:
-                    g = first[:]
-                else:
-                    g = fetch5(t, halves[1], "g5_%d" % (t - 1))[:]
+                g = g5[:, halves[h]]
+                if last and h == 1:
+                    g = before[:, halves[h]]
+                    fetch5(t, halves[h], g)
                 nc.vector.tensor_tensor(diff[t // 2][h][:, t % 2, :], pw[t][:, halves[h]], g, ALU.subtract)
             if t % 2 == 1:
                 for h in range(2):
                     pair = diff[t // 2][h][:].rearrange("p t c -> p c t")
-                    nc.vector.scalar_tensor_tensor(hid[h][:, :, t - 1:t + 1], pair, -1.0, pair, ALU.mult, ALU.max)
+                    if last and h == 0:
+                        nc.scalar.activation(hid[h][:, :, t - 1:t + 1], pair, ABS)
+                    else:
+                        nc.vector.scalar_tensor_tensor(hid[h][:, :, t - 1:t + 1], pair, -1.0, pair, ALU.mult, ALU.max)
 
         for h in range(2):
             codes = sbuf("hid_codes%d" % h, [P, HALF], U32)
@@ -171,9 +180,9 @@ def tile_picked_tokens_store_one_wholepage_further_plain_kernel(
                     y[h][b][:], lhsT=wb_codes[:, rows].bitcast(FP8X4), lhsT_scale=wb_plane[:, rows],
                     rhs=codes[:].bitcast(FP8X4), rhs_scale=scales[:], start=False, stop=True)
                 res = sbuf("res%d%d" % (h, b), [P, HALF], F32)
-                if b == 0:
-                    nc.scalar.copy(res[:], y[h][b][:])
-                    nc.scalar.dma_start(out[rows, h * HALF:(h + 1) * HALF], res[:])
-                else:
+                if (h, b) == (1, 0):
                     nc.vector.tensor_copy(res[:], y[h][b][:])
-                    nc.sync.dma_start(out[rows, h * HALF:(h + 1) * HALF], res[:])
+                else:
+                    nc.scalar.copy(res[:], y[h][b][:])
+                queue = nc.scalar if (h, b) == (1, 1) else nc.sync
+                queue.dma_start(out[rows, h * HALF:(h + 1) * HALF], res[:])

from contextlib import ExitStack

import concourse.mybir as mybir

K, J, R, T, F, O, C, N = 512, 512, 512, 1024, 1024, 192, 256, 256
FLOPS = 2 * K * R * J + 2 * R * N * C + 2 * K * N * C

F32 = mybir.dt.float32
BF16 = mybir.dt.bfloat16
I32 = mybir.dt.int32
U32 = mybir.dt.uint32
U16 = mybir.dt.uint16
U8 = mybir.dt.uint8
FP8X4 = mybir.dt.float8_e4m3fn_x4
FP4X4 = mybir.dt.float4_e2m1fn_x4
ALU = mybir.AluOpType
COPY = mybir.ActivationFunctionType.Copy
ABS = mybir.ActivationFunctionType.Abs

P = 128
PACK = 4
GROUP = 16
HALF = C // 2


def tile_picked_tokens_store_one_wholepage_further_plain_kernel(
    tc, xt_words, xt_scales, wt_words, wt_scales, sa, sb, wb_words, wb_scales, ws_words, ws_scales,
    offs, offs2, offs3, offs4, offs5, offs6, out,
):
    nc = tc.nc
    with ExitStack() as ctx:
        keep = ctx.enter_context(tc.tile_pool(name="keep", bufs=1))
        psum = ctx.enter_context(tc.psum_pool(name="psum", bufs=1))

        def sbuf(name, shape, dtype, tag=None):
            return keep.tile(shape, dtype, name=name, tag=tag or name, align_bytes=64)

        def load_list(name, src):
            tile = sbuf(name, list(src.shape), U16)
            nc.sync.dma_start(tile[:], src)
            return tile

        def load_words(name, src, shape, dtype):
            tile = sbuf(name, shape, dtype)
            nc.sync.dma_start(tile[:].bitcast(I32), src.bitcast(I32))
            return tile

        def cleared_plane(name, width, engine):
            plane = sbuf(name, [P, width], U8)
            engine.memset(plane[:].bitcast(I32), 0)
            return plane

        def load_plane(plane, src):
            for q in range(4):
                nc.sync.dma_start(plane[32 * q:32 * q + 4, :].bitcast(I32), src[0, 4 * q:4 * q + 4, :].bitcast(I32))

        wt_plane = cleared_plane("wt_plane", F, nc.vector)
        xt_plane = cleared_plane("xt_plane", T, nc.gpsimd)
        pw = [sbuf("pw%d" % t, [P, C], F32) for t in range(PACK)]
        for t in range(PACK):
            nc.vector.memset(pw[t][:], 0.0)
        ws_plane = cleared_plane("ws_plane", N, nc.vector)
        wb_plane = cleared_plane("wb_plane", N, nc.vector)

        wt_win = load_words("wt_win", wt_words[0], [P, F], U16)
        list2 = load_list("list2", offs2)
        list1 = load_list("list1", offs)
        xt_win = load_words("xt_win", xt_words[0], [P, T], U16)
        load_plane(wt_plane, wt_scales)
        load_plane(xt_plane, xt_scales)
        list3 = load_list("list3", offs3)
        sa_t = sbuf("sa_t", [P, PACK], F32)
        nc.gpsimd.dma_start(sa_t[:], sa.rearrange("(p t) o -> p (t o)", t=PACK))
        list5 = load_list("list5", offs5)
        sb_t = sbuf("sb_t", [P, PACK], F32)
        nc.gpsimd.dma_start(sb_t[:], sb.rearrange("(p t) o -> p (t o)", t=PACK))
        list4 = load_list("list4", offs4)
        list6 = load_list("list6", offs6)
        ws_codes = load_words("ws_codes", ws_words[0].rearrange("p n t -> p (n t)"), [P, N], U32)
        load_plane(ws_plane, ws_scales)
        wb_codes = load_words("wb_codes", wb_words[0].rearrange("p n t -> p (n t)"), [P, N], U32)
        load_plane(wb_plane, wb_scales)

        wt_got = sbuf("wt_got", [P, R], U16)
        nc.vector.tensor_copy(wt_got[:], wt_win[:].indirect(list2[:]))
        wt_dealt = {}
        wt_bytes = wt_got[:].bitcast(U8).rearrange("p (m t b) -> p m t b", t=PACK, b=2)

        def deal(t0, t1):
            tile = sbuf("wt_dealt%d" % t0, [P, t1 - t0, P], U16, tag="wt_dealt")
            nc.vector.tensor_copy(tile[:], wt_got[:].rearrange("p (m t) -> p t m", t=PACK)[:, t0:t1, :])
            for t in range(t0, t1):
                wt_dealt[t] = tile[:, t - t0, :]

        wt_sc = sbuf("wt_sc", [P, PACK, P], U8)
        x_codes = sbuf("x_codes", [P, J], U16)
        x_sc = sbuf("x_sc", [P, J], U8)
        a = [sbuf("a%d" % t, [P, J], F32) for t in range(PACK)]

        def first_product(t, cols, tag):
            bank = psum.tile([P, cols.stop - cols.start], F32, name="acc_" + tag, tag=tag)
            nc.tensor.matmul_mx(
                bank[:], lhsT=wt_dealt[t].bitcast(U8).bitcast(FP4X4), lhsT_scale=wt_sc[:, t, :],
                rhs=x_codes[:, cols].bitcast(U8).bitcast(FP4X4), rhs_scale=x_sc[:, cols], start=True, stop=True)
            return bank

        nc.vector.tensor_copy(x_codes[:], xt_win[:].indirect(list1[:]))
        deal(0, 1)
        nc.vector.tensor_copy(wt_sc[:].rearrange("p t m -> p m t"), wt_plane[:].indirect(list2[:]))
        for i, cols in enumerate((slice(0, 256), slice(256, 384), slice(384, J))):
            entries = list1[:, cols.start // GROUP:cols.stop // GROUP]
            nc.vector.tensor_copy(x_sc[:, cols], xt_plane[:].indirect(entries))
            bank = first_product(0, cols, "a_part%d" % i)
            if cols.stop < J:
                nc.scalar.copy(a[0][:, cols], bank[:])
            else:
                nc.vector.tensor_copy(a[0][:, cols], bank[:])
        deal(1, PACK)
        for t in range(1, PACK):
            bank = first_product(t, slice(0, J), "a_tile%d" % t)
            nc.vector.tensor_copy(a[t][:], bank[:])

        x6_codes = sbuf("x6_codes", [P, C], U16, tag="wt_got")
        x6_sc = sbuf("x6_sc", [P, C], U8, tag="wt_dealt")
        nc.vector.tensor_copy(x6_codes[:], xt_win[:].indirect(list6[:]))
        nc.vector.tensor_copy(x6_sc[:], xt_plane[:].indirect(list6[:]))
        y = [[psum.tile([P, HALF], F32, name="y%d%d" % (h, b), tag=("a_part%d" % b if h else "y%d" % b)) for b in range(2)] for h in range(2)]
        for h in range(2):
            cols = slice(h * HALF, (h + 1) * HALF)
            for b in range(2):
                rows = slice(b * P, (b + 1) * P)
                nc.tensor.matmul_mx(
                    y[h][b][:], lhsT=ws_codes[:, rows].bitcast(FP8X4), lhsT_scale=ws_plane[:, rows],
                    rhs=x6_codes[:, cols].bitcast(U8).bitcast(FP4X4), rhs_scale=x6_sc[:, cols], start=True, stop=False)

        held = {(0, 0): "wt_sc", (0, 1): "x_codes"}
        diff = [[sbuf("diff%d%d" % (u, h), [P, 2, HALF], F32, tag=held.get((u, h))) for h in range(2)] for u in range(2)]
        hid = [sbuf("hid%d" % h, [P, HALF, PACK], BF16) for h in range(2)]

        def fetch5(t, cols, dst):
            entries = list5[:, cols.start // GROUP:cols.stop // GROUP]
            nc.scalar.activation(dst, a[t][:].indirect(entries), COPY, scale=sb_t[:, t:t + 1])

        halves = (slice(0, HALF), slice(HALF, C))
        for t in range(PACK):
            last = t == PACK - 1
            if t == 0:
                h1 = sbuf("h1_first", [P, O], F32, tag="fetched")[:]
                g5 = sbuf("g5_first", [P, C], F32)[:]
            else:
                if t == 1:
                    rest = sbuf("fetched_rest", [P, PACK - 1, O + C], F32, tag="fetched")
                before = g5
                h1, g5 = rest[:, t - 1, :O], rest[:, t - 1, O:]
            nc.scalar.activation(h1, a[t][:].indirect(list3[:]), COPY, scale=sa_t[:, t:t + 1])
            cols = halves[0] if last else slice(0, C)
            fetch5(t, cols, g5[:, cols])
            nc.scalar.activation(pw[t][:].indirect(list4[:]), h1, COPY)
            for h in range(2):
                g = g5[:, halves[h]]
                if last and h == 1:
                    g = before[:, halves[h]]
                    fetch5(t, halves[h], g)
                nc.vector.tensor_tensor(diff[t // 2][h][:, t % 2, :], pw[t][:, halves[h]], g, ALU.subtract)
            if t % 2 == 1:
                for h in range(2):
                    pair = diff[t // 2][h][:].rearrange("p t c -> p c t")
                    if last and h == 0:
                        nc.scalar.activation(hid[h][:, :, t - 1:t + 1], pair, ABS)
                    else:
                        nc.vector.scalar_tensor_tensor(hid[h][:, :, t - 1:t + 1], pair, -1.0, pair, ALU.mult, ALU.max)

        for h in range(2):
            codes = sbuf("hid_codes%d" % h, [P, HALF], U32)
            scales = sbuf("hid_sc%d" % h, [P, HALF], U8)
            nc.vector.quantize_mx(codes[:].bitcast(FP8X4), scales[:], hid[h][:].rearrange("p c t -> p (c t)"))
            for b in range(2):
                rows = slice(b * P, (b + 1) * P)
                nc.tensor.matmul_mx(
                    y[h][b][:], lhsT=wb_codes[:, rows].bitcast(FP8X4), lhsT_scale=wb_plane[:, rows],
                    rhs=codes[:].bitcast(FP8X4), rhs_scale=scales[:], start=False, stop=True)
                res = sbuf("res%d%d" % (h, b), [P, HALF], F32)
                if (h, b) == (1, 0):
                    nc.vector.tensor_copy(res[:], y[h][b][:])
                else:
                    nc.scalar.copy(res[:], y[h][b][:])
                queue = nc.scalar if (h, b) == (1, 1) else nc.sync
                queue.dma_start(out[rows, h * HALF:(h + 1) * HALF], res[:])
